import numpy as np
import ml_dtypes


def mxq(x, axis, fmt="e4m3"):
    dtype, down = {"e4m3": (ml_dtypes.float8_e4m3fn, 7), "e5m2": (ml_dtypes.float8_e5m2, 14)}[fmt]
    v = np.moveaxis(np.asarray(x, np.float32).astype(ml_dtypes.bfloat16).astype(np.float64), axis, -1)
    blocks = v.reshape(v.shape[:-1] + (-1, 32))
    amax = np.abs(blocks).max(-1, keepdims=True)
    byte = np.maximum(np.where(amax > 0, np.frexp(amax)[1] - 1 + 127, 0) - down, 1)
    scale = np.exp2(byte - 127.0)
    codes = (blocks / scale).astype(np.float32).astype(dtype).astype(np.float64)
    return np.moveaxis((codes * scale).reshape(v.shape), -1, axis)


WIDE = False


def mx_kscale(k):
    if not WIDE:
        return np.ones(k)
    levels = np.array([10, -10, 5, -5, 0])
    if k % 512:
        return np.exp2(np.random.permutation(np.resize(levels, k // 32))).repeat(32)
    a = np.empty((k // 512, 16))
    for p in range(k // 512):
        a[p, :8] = np.random.permutation(np.resize(levels, 8))
        for g in range(8):
            far = levels[np.abs(levels - a[p, g]) >= 10]
            a[p, g + 8] = far[np.random.randint(len(far))]
    return np.exp2(a.ravel()).repeat(32)


def f64(x):
    return np.asarray(x).astype(np.float64)


def striped(idx):
    return np.tile(idx.reshape(-1, 16).T, (8, 1)).astype(np.uint16)


def unstriped(offs):
    return offs[:16].T.reshape(-1).astype(np.int64)


E2M1 = np.array([0.0, 0.5, 1.0, 1.5, 2.0, 3.0, 4.0, 6.0, -0.0, -0.5, -1.0, -1.5, -2.0, -3.0, -4.0, -6.0])


def pack_weight(w, fmt):
    k, n = w.shape
    w = f64(np.asarray(w, np.float32).astype(ml_dtypes.bfloat16)).reshape(k // 32, 32, n)
    amax = np.abs(w).max(1)
    if fmt == "e4m3":
        byte = np.frexp(amax)[1] - 1 + 127 - 7
    else:
        mant, ex = np.frexp(amax / 6.0)
        byte = np.where(mant > 0.5, ex, ex - 1) + 127
    byte = np.clip(np.where(amax > 0, byte, 1), 1, 254)
    scaled = (w * np.exp2(127.0 - byte)[:, None, :]).reshape(k, n).astype(np.float32)
    by_word = np.ascontiguousarray(scaled.reshape(k // 512, 128, 4, n).transpose(0, 1, 3, 2))
    if fmt == "e4m3":
        words = by_word.astype(ml_dtypes.float8_e4m3fn).view(np.uint8)
    else:
        c = by_word.astype(ml_dtypes.float4_e2m1fn).view(np.uint8) & 0xF
        words = (c[..., 0::2] | (c[..., 1::2] << 4)).reshape(k // 512, 128, 2 * n)
    return np.ascontiguousarray(words), np.ascontiguousarray(byte.astype(np.uint8).reshape(k // 512, 16, n))


def unpack_weight(words, scales, fmt):
    g, _, n = scales.shape
    words = np.ascontiguousarray(words).reshape(g, 128, n, -1)
    if fmt == "e4m3":
        vals = words.view(ml_dtypes.float8_e4m3fn).astype(np.float64)
    else:
        nib = np.empty((g, 128, n, 4), np.uint8)
        nib[..., 0::2] = words & 0xF
        nib[..., 1::2] = words >> 4
        vals = E2M1[nib]
    vals = vals * np.repeat(np.exp2(scales.astype(np.float64) - 127.0), 8, axis=1)[..., None]
    return vals.transpose(0, 1, 3, 2).reshape(g * 512, n)


def gelu(v):
    return 0.5 * v * (1.0 + np.tanh(np.sqrt(2.0 / np.pi) * (v + 0.044715 * v**3)))


K, K2, H, N, T, T2, S = 1024, 512, 1024, 512, 4096, 2048, 1024

def setup_inputs():
    n = np.random.standard_normal
    s = mx_kscale(K)[:, None]
    s2 = mx_kscale(K2)[:, None]
    u = mx_kscale(H)[:, None]
    tab_words, tab_scales = pack_weight(n((K, T)) * s, "e4m3")
    tab2_words, tab2_scales = pack_weight(n((K2, T2)) * s2, "e4m3")
    w2_words, w2_scales = pack_weight(n((K2, H)) / np.sqrt(K2) / s2, "e2m1")
    return {
        "tab_words": tab_words, "tab_scales": tab_scales,
        "tab2_words": tab2_words, "tab2_scales": tab2_scales,
        "offs": striped(np.random.permutation(T)[:S]),
        "offs2": striped(np.random.permutation(T2)[:S]),
        "w1": (n((K, H)) / np.sqrt(K) / s * u.T).astype(np.float32),
        "w2_words": w2_words, "w2_scales": w2_scales,
        "bi": (0.5 * n(H)).astype(np.float32),
        "wr": (1.5 * n((H, N)) / np.sqrt(H) / u).astype(np.float32),
        "base": (0.5 * n(N)).astype(np.float32),
    }

def reference(tab_words, tab_scales, tab2_words, tab2_scales, offs, offs2, w1, w2_words, w2_scales, bi, wr, base):
    v = unpack_weight(tab_words, tab_scales, "e4m3")[:, unstriped(offs)]
    v2 = unpack_weight(tab2_words, tab2_scales, "e4m3")[:, unstriped(offs2)]
    w2 = unpack_weight(w2_words, w2_scales, "e2m1")
    a = mxq(f64(w1), 0, "e4m3").T @ v
    b = (w2.T @ v2) + f64(bi)[:, None]
    h = a / (1.0 + np.abs(b))
    y = mxq(f64(wr), 0, "e4m3").T @ mxq(h, 0, "e4m3")
    return y + f64(base)[:, None]

@@ -1,0 +1,315 @@
+from contextlib import ExitStack
+
+import concourse.mybir as mybir
+
+K, K2, H, N, T, T2, S = 1024, 512, 1024, 512, 4096, 2048, 1024
+FLOPS = 2 * (K * H * S + K2 * H * S + H * N * S)
+
+F32 = mybir.dt.float32
+BF16 = mybir.dt.bfloat16
+I32 = mybir.dt.int32
+U32 = mybir.dt.uint32
+U16 = mybir.dt.uint16
+U8 = mybir.dt.uint8
+FP8X4 = mybir.dt.float8_e4m3fn_x4
+FP4X4 = mybir.dt.float4_e2m1fn_x4
+ACT = mybir.ActivationFunctionType
+ALU = mybir.AluOpType
+
+P = 128
+PACK = 4
+KP = P * PACK
+HALF = 512
+AW = 128
+YW = 256
+TAB_ROW = 8
+CAST_ENG = "gvgggg"
+SQ_ENG = "ssssssss"
+EVAC_ENG = "vsvsvsvs"
+
+
+def tile_list_inhibited_drug_response_kernel(tc, tab_words, tab_scales, tab2_words, tab2_scales, offs, offs2,
+                                                      w1, w2_words, w2_scales, bi, wr, base, out):
+    nc = tc.nc
+    with ExitStack() as ctx:
+        keep = ctx.enter_context(tc.tile_pool(name="keep", bufs=1))
+        ring = ctx.enter_context(tc.tile_pool(name="ring", bufs=1))
+        stage = ctx.enter_context(tc.tile_pool(name="stage", bufs=2))
+        psum = ctx.enter_context(tc.psum_pool(name="psum", bufs=4))
+
+        def held(shape, dtype, name, place=None):
+            if place is None:
+                return keep.tile(shape, dtype, name=name, align_bytes=64)
+            return ring.tile(shape, dtype, name=name, align_bytes=64, offset=place)
+
+        list1 = held([P, S // 16], U16, "list1")
+        list2 = held([P, S // 16], U16, "list2")
+        w2w_raw = held([P, H // 2], I32, "w2w_raw", 16384)
+        w2s_raw = held([P, H // 4], I32, "w2s_raw", 27584)
+        t2s = held([P, T2 // 4], I32, "t2s", 45056)
+        t2w = held([P, T2], I32, "t2w", 53248)
+        w2w = held([P, 2 * H], U8, "w2w")
+        w2s = held([P, H], U8, "w2s")
+        bi_sb = held([P, 2, PACK], F32, "bi_sb")
+        base_sb = held([P, N // P], F32, "base_sb")
+        warm = held([P, 1], F32, "warm", 0)
+        t1w, w1_raw, wr_raw = {}, {}, {}
+        w1c = [[held([P, KP], U32, f"w1c{g}{a}") for a in range(2)] for g in range(2)]
+        w1s = [[held([P, KP], U8, f"w1s{g}{a}") for a in range(2)] for g in range(2)]
+        wrc = [held([P, N], U32, f"wrc{g}") for g in range(2)]
+        wrs = [held([P, N], U8, f"wrs{g}") for g in range(2)]
+        v2w, v2s = {}, {}
+        v1w = [[held([P, HALF], U32, f"v1w{a}{h}") for h in range(2)] for a in range(2)]
+        v1s = [held([P, HALF], U8, f"v1s{h}") for h in range(2)]
+        gate = [[held([P, PACK, HALF], F32, f"gate{g}{h}") for h in range(2)] for g in range(2)]
+        hc = [[held([P, YW], U32, f"hc{g}{q}") for q in range(S // YW)] for g in range(2)]
+        hs = [[held([P, YW], U8, f"hs{g}{q}") for q in range(S // YW)] for g in range(2)]
+
+        nc.vector.memset(warm[:], 1.0)
+        nc.vector.memset(t2s[:], 0)
+        nc.vector.memset(w2s_raw[:], 0)
+        nc.scalar.activation(out=warm[:], in_=warm[:], func=ACT.Abs_reciprocal_sqrt)
+
+        def load_scale_rows(queue, tile, rows, q):
+            queue.dma_start(out=tile[32 * q:32 * q + 4, :], in_=rows[4 * q:4 * q + 4, :].bitcast(I32))
+
+        def load_words(tile, words):
+            nc.sync.dma_start(out=tile[:], in_=words.rearrange("p t i -> p (t i)").bitcast(I32))
+
+        def load_rows(tile, rows):
+            nc.sync.dma_start(out=tile[:], in_=rows.rearrange("(p j) c -> p j c", j=PACK))
+
+        def load_t1w(a, slot):
+            t1w[a] = held([P, T], I32, f"t1w{a}", slot)
+            load_words(t1w[a], tab_words[a])
+
+        def load_t1s(slot):
+            tile = held([P, T // 4], I32, "t1s", slot)
+            nc.vector.memset(tile[:], 0)
+            for q in range(4):
+                p0 = 32 * q + TAB_ROW
+                nc.sync.dma_start(out=tile[p0:p0 + 8, :], in_=tab_scales[:, 4 * q:4 * q + 4, :].bitcast(I32))
+            return tile
+
+        def load_w1(g, a, slot):
+            w1_raw[g, a] = held([P, PACK, KP], F32, f"w1raw{g}{a}", slot)
+            load_rows(w1_raw[g, a], w1[a * KP:(a + 1) * KP, g * KP:(g + 1) * KP])
+
+        def load_wr(g, slot):
+            wr_raw[g] = held([P, PACK, N], F32, f"wrraw{g}", slot)
+            load_rows(wr_raw[g], wr[g * KP:(g + 1) * KP, :])
+
+        nc.sync.dma_start(list2[:], offs2)
+        nc.sync.dma_start(list1[:], offs)
+        nc.sync.dma_start(out=bi_sb[:], in_=bi.rearrange("(g p t) -> p g t", g=2, t=PACK))
+        nc.sync.dma_start(out=base_sb[:], in_=base.rearrange("(p c) -> p c", c=PACK))
+        nc.sync.dma_start(out=w2w_raw[:], in_=w2_words[0].bitcast(I32))
+        for q in range(2):
+            load_scale_rows(nc.sync, t2s, tab2_scales[0], q)
+        load_words(t2w, tab2_words[0])
+        for q in range(2, 4):
+            load_scale_rows(nc.sync, t2s, tab2_scales[0], q)
+        for q in range(4):
+            load_scale_rows(nc.sync, w2s_raw, w2_scales[0], q)
+
+        def order_w2_words(g):
+            cols = slice(g * KP, (g + 1) * KP)
+            nc.vector.tensor_copy(out=w2w[:].bitcast(U16)[:, cols].rearrange("p (t m) -> p m t", t=PACK),
+                                  in_=w2w_raw[:].bitcast(U16)[:, cols].rearrange("p (m t) -> p m t", t=PACK))
+
+        def order_w2_scales(g):
+            cols = slice(g * KP, (g + 1) * KP)
+            nc.vector.tensor_copy(out=w2s[:, cols].rearrange("p (t m) -> p m t", t=PACK),
+                                  in_=w2s_raw[:].bitcast(U8)[:, cols].rearrange("p (m t) -> p m t", t=PACK))
+
+        def gather(dst, window, offsets, j0, j1):
+            nc.vector.tensor_copy(dst, window.indirect(offsets[:, j0 // 16:j1 // 16]))
+
+        def gather2s(j0, j1, place):
+            v2s[j0] = held([P, j1 - j0], U8, f"v2s{j0}", place)
+            gather(v2s[j0][:], t2s[:].bitcast(U8), list2, j0, j1)
+
+        def gather2w(j0, j1, place):
+            v2w[j0] = held([P, j1 - j0], U32, f"v2w{j0}", place)
+            gather(v2w[j0][:], t2w[:].bitcast(U32), list2, j0, j1)
+
+        def gather1s(t1s, h):
+            gather(v1s[h][:], t1s[:].bitcast(U8), list1, h * HALF, (h + 1) * HALF)
+
+        def gather1w(a, h):
+            gather(v1w[a][h][:], t1w[a][:].bitcast(U32), list1, h * HALF, (h + 1) * HALF)
+
+        def round_copy(eng, dst, src):
+            if eng == "v":
+                nc.vector.tensor_copy(out=dst, in_=src)
+            elif eng == "s":
+                nc.scalar.copy(out=dst, in_=src)
+            else:
+                nc.gpsimd.tensor_scalar(out=dst, in0=src, scalar1=1.0, scalar2=0.0, op0=ALU.mult, op1=ALU.add)
+
+        def quantize(codes, scales, values):
+            nc.vector.quantize_mx(out=codes[:].bitcast(FP8X4), scales=scales[:], in_=values[:])
+
+        def cast(eng, raw):
+            grouped = stage.tile([P, PACK * KP], BF16, name="grouped", bufs=4, align_bytes=64)
+            order = "p m j t" if eng == "v" else "p m t j"
+            dst = grouped[:].rearrange("p (t m j) -> " + order, t=PACK, j=PACK)
+            src = raw[:].rearrange("p j (m t) -> " + order, t=PACK)
+            step = P if eng == "v" else P // 2
+            for m0 in range(0, P, step):
+                round_copy(eng, dst[:, m0:m0 + step], src[:, m0:m0 + step])
+            return grouped
+
+        def cast_w1(g, a):
+            return cast(CAST_ENG[2 * g + a], w1_raw[g, a])
+
+        def cast_wr(g):
+            return cast(CAST_ENG[4 + g], wr_raw[g])
+
+        def load_gate(g, j0, j1):
+            h, c0 = divmod(j0, HALF)
+            width = j1 - j0
+            piece = 0 if j0 < YW else YW
+            cols = slice(j0 - piece, j1 - piece)
+            for t in range(PACK):
+                col = g * KP + t * P
+                bank = psum.tile([P, width], F32, name="by")
+                nc.tensor.matmul_mx(out=bank[:], lhsT=w2w[:, 2 * col:2 * (col + P)].bitcast(FP4X4),
+                                    lhsT_scale=w2s[:, col:col + P], rhs=v2w[piece][:, cols].bitcast(FP8X4),
+                                    rhs_scale=v2s[piece][:, cols], start=True, stop=True)
+                nc.scalar.activation(out=gate[g][h][:, t, c0:c0 + width], in_=bank[:], func=ACT.Abs,
+                                     bias=bi_sb[:, g, t:t + 1])
+
+        def gate_part(g, q):
+            h, c0 = divmod(q * YW, HALF)
+            return gate[g][h][:, :, c0:c0 + YW]
+
+        def root_gate(g, q):
+            nc.scalar.activation(out=gate_part(g, q), in_=gate_part(g, q), func=ACT.Abs_reciprocal_sqrt, bias=1.0)
+
+        def square_gate(g, q):
+            part = gate_part(g, q)
+            if SQ_ENG[4 * g + q] == "s":
+                nc.scalar.activation(out=part, in_=part, func=ACT.Square)
+            else:
+                nc.vector.tensor_tensor(out=part, in0=part, in1=part, op=ALU.mult)
+
+        def drive(g, q):
+            hb = stage.tile([P, YW * PACK], BF16, name="hb", bufs=3, align_bytes=64)
+            for u in range(YW // AW):
+                h, c0 = divmod(q * YW + u * AW, HALF)
+                bank = psum.tile([P, PACK, AW], F32, name="abank")
+                for t in range(PACK):
+                    for a in range(2):
+                        nc.tensor.matmul_mx(out=bank[:, t, :], lhsT=w1c[g][a][:, t * P:(t + 1) * P].bitcast(FP8X4),
+                                            lhsT_scale=w1s[g][a][:, t * P:(t + 1) * P],
+                                            rhs=v1w[a][h][:, c0:c0 + AW].bitcast(FP8X4),
+                                            rhs_scale=v1s[h][TAB_ROW + 4 * a:, c0:c0 + AW],
+                                            start=(a == 0), stop=(a == 1))
+                nc.vector.tensor_tensor(
+                    out=hb[:, u * AW * PACK:(u + 1) * AW * PACK].rearrange("p (c i t) -> p c t i", i=4, t=PACK),
+                    in0=bank[:].rearrange("p t (c i) -> p c t i", i=4),
+                    in1=gate[g][h][:, :, c0:c0 + AW].rearrange("p t (c i) -> p c t i", i=4),
+                    op=ALU.mult)
+            return hb
+
+        def read_out(q):
+            res = stage.tile([P, N // P, YW], F32, name="res", bufs=3)
+            for pair in range(2):
+                bank = psum.tile([P, 2, YW], F32, name="by")
+                for e in range(2):
+                    c = 2 * pair + e
+                    for g in range(2):
+                        nc.tensor.matmul_mx(out=bank[:, e, :], lhsT=wrc[g][:, c * P:(c + 1) * P].bitcast(FP8X4),
+                                            lhsT_scale=wrs[g][:, c * P:(c + 1) * P],
+                                            rhs=hc[g][q][:].bitcast(FP8X4), rhs_scale=hs[g][q][:],
+                                            start=(g == 0), stop=(g == 1))
+                for e in range(2):
+                    c = 2 * pair + e
+                    if EVAC_ENG[2 * q + pair] == "s":
+                        nc.scalar.activation(out=res[:, c, :], in_=bank[:, e, :], func=ACT.Identity,
+                                             bias=base_sb[:, c:c + 1])
+                    else:
+                        nc.vector.tensor_scalar(out=res[:, c, :], in0=bank[:, e, :], scalar1=base_sb[:, c:c + 1],
+                                                scalar2=None, op0=ALU.add)
+                nc.sync.dma_start(
+                    out=out[:, q * YW:(q + 1) * YW].rearrange("(p c) j -> p c j", c=PACK)[:, 2 * pair:2 * pair + 2, :],
+                    in_=res[:, 2 * pair:2 * pair + 2, :])
+
+        load_t1w(0, 0)
+        order_w2_words(0)
+        order_w2_words(1)
+        t1s = load_t1s(16384)
+        order_w2_scales(0)
+        gather2s(0, 256, None)
+        gather2w(0, 256, None)
+        load_gate(0, 0, 256)
+        order_w2_scales(1)
+        load_t1w(1, 28416)
+        load_gate(1, 0, 256)
+        root_gate(0, 0)
+        gather2s(256, 1024, 27648)
+        load_w1(0, 0, 45056)
+        gather2w(256, 1024, 24576)
+        load_w1(0, 1, 53248)
+        root_gate(1, 0)
+        square_gate(0, 0)
+        square_gate(1, 0)
+        load_gate(0, 256, 512)
+        load_gate(0, 512, 1024)
+        for h in range(2):
+            gather1w(0, h)
+        for h in range(2):
+            gather1s(t1s, h)
+        load_w1(1, 0, 16384)
+        for h in range(2):
+            gather1w(1, h)
+        load_w1(1, 1, 28416)
+        root_gate(0, 1)
+        root_gate(0, 2)
+        square_gate(0, 1)
+        root_gate(0, 3)
+        load_gate(1, 256, 512)
+        square_gate(0, 2)
+        square_gate(0, 3)
+        root_gate(1, 1)
+        load_gate(1, 512, 1024)
+        square_gate(1, 1)
+        root_gate(1, 2)
+        root_gate(1, 3)
+        square_gate(1, 2)
+        square_gate(1, 3)
+        g00 = cast_w1(0, 0)
+        load_wr(0, 45056)
+        g01 = cast_w1(0, 1)
+        load_wr(1, 53248)
+        quantize(w1c[0][0], w1s[0][0], g00)
+        quantize(w1c[0][1], w1s[0][1], g01)
+        g10 = cast_w1(1, 0)
+        g11 = cast_w1(1, 1)
+        h0 = drive(0, 0)
+        h1 = drive(0, 1)
+        quantize(hc[0][0], hs[0][0], h0)
+        h2 = drive(0, 2)
+        quantize(hc[0][1], hs[0][1], h1)
+        quantize(w1c[1][0], w1s[1][0], g10)
+        h3 = drive(0, 3)
+        quantize(hc[0][2], hs[0][2], h2)
+        quantize(w1c[1][1], w1s[1][1], g11)
+        r0 = cast_wr(0)
+        r1 = cast_wr(1)
+        h0 = drive(1, 0)
+        quantize(hc[0][3], hs[0][3], h3)
+        quantize(wrc[0], wrs[0], r0)
+        h1 = drive(1, 1)
+        quantize(hc[1][0], hs[1][0], h0)
+        quantize(wrc[1], wrs[1], r1)
+        read_out(0)
+        h2 = drive(1, 2)
+        quantize(hc[1][1], hs[1][1], h1)
+        read_out(1)
+        h3 = drive(1, 3)
+        quantize(hc[1][2], hs[1][2], h2)
+        read_out(2)
+        quantize(hc[1][3], hs[1][3], h3)
+        read_out(3)

@@ -23,9 +23,9 @@ HALF = 512
 AW = 128
 YW = 256
 TAB_ROW = 8
-CAST_ENG = "gvgggg"
+CAST_ENG = "vvvvvv"
 SQ_ENG = "ssssssss"
-EVAC_ENG = "vsvsvsvs"
+EVAC_ENG = ""
 
 
 def tile_list_inhibited_drug_response_kernel(tc, tab_words, tab_scales, tab2_words, tab2_scales, offs, offs2,
@@ -44,29 +44,29 @@ def tile_list_inhibited_drug_response_kernel(tc, tab_words, tab_scales, tab2_wor
 
         list1 = held([P, S // 16], U16, "list1")
         list2 = held([P, S // 16], U16, "list2")
-        w2w_raw = held([P, H // 2], I32, "w2w_raw", 16384)
-        w2s_raw = held([P, H // 4], I32, "w2s_raw", 27584)
-        t2s = held([P, T2 // 4], I32, "t2s", 45056)
-        t2w = held([P, T2], I32, "t2w", 53248)
+        w2w_raw = held([P, H // 2], I32, "w2w_raw")
+        w2s_raw = held([P, H // 4], I32, "w2s_raw", 48064)
+        t2s = held([P, T2 // 4], I32, "t2s", 28416)
+        t2w = held([P, T2], I32, "t2w", 56384)
         w2w = held([P, 2 * H], U8, "w2w")
         w2s = held([P, H], U8, "w2s")
         bi_sb = held([P, 2, PACK], F32, "bi_sb")
         base_sb = held([P, N // P], F32, "base_sb")
-        warm = held([P, 1], F32, "warm", 0)
+        warm = held([P, 32], F32, "warm", 16320)
         t1w, w1_raw, wr_raw = {}, {}, {}
         w1c = [[held([P, KP], U32, f"w1c{g}{a}") for a in range(2)] for g in range(2)]
         w1s = [[held([P, KP], U8, f"w1s{g}{a}") for a in range(2)] for g in range(2)]
         wrc = [held([P, N], U32, f"wrc{g}") for g in range(2)]
         wrs = [held([P, N], U8, f"wrs{g}") for g in range(2)]
         v2w, v2s = {}, {}
-        v1w = [[held([P, HALF], U32, f"v1w{a}{h}") for h in range(2)] for a in range(2)]
-        v1s = [held([P, HALF], U8, f"v1s{h}") for h in range(2)]
+        v1w = [held([P, S], U32, f"v1w{a}") for a in range(2)]
+        v1s = held([P, S], U8, "v1s")
         gate = [[held([P, PACK, HALF], F32, f"gate{g}{h}") for h in range(2)] for g in range(2)]
-        hc = [[held([P, YW], U32, f"hc{g}{q}") for q in range(S // YW)] for g in range(2)]
-        hs = [[held([P, YW], U8, f"hs{g}{q}") for q in range(S // YW)] for g in range(2)]
+        hc = [held([P, S], U32, f"hc{g}") for g in range(2)]
+        hs = [held([P, S], U8, f"hs{g}") for g in range(2)]
 
-        nc.vector.memset(warm[:], 1.0)
         nc.vector.memset(t2s[:], 0)
+        nc.vector.memset(warm[:], 1.0)
         nc.vector.memset(w2s_raw[:], 0)
         nc.scalar.activation(out=warm[:], in_=warm[:], func=ACT.Abs_reciprocal_sqrt)
 
@@ -102,25 +102,23 @@ def tile_list_inhibited_drug_response_kernel(tc, tab_words, tab_scales, tab2_wor
         nc.sync.dma_start(list2[:], offs2)
         nc.sync.dma_start(list1[:], offs)
         nc.sync.dma_start(out=bi_sb[:], in_=bi.rearrange("(g p t) -> p g t", g=2, t=PACK))
-        nc.sync.dma_start(out=base_sb[:], in_=base.rearrange("(p c) -> p c", c=PACK))
-        nc.sync.dma_start(out=w2w_raw[:], in_=w2_words[0].bitcast(I32))
-        for q in range(2):
+        for q in range(4):
             load_scale_rows(nc.sync, t2s, tab2_scales[0], q)
         load_words(t2w, tab2_words[0])
-        for q in range(2, 4):
-            load_scale_rows(nc.sync, t2s, tab2_scales[0], q)
+        nc.sync.dma_start(out=w2w_raw[:], in_=w2_words[0].bitcast(I32))
         for q in range(4):
             load_scale_rows(nc.sync, w2s_raw, w2_scales[0], q)
+        nc.sync.dma_start(out=base_sb[:], in_=base.rearrange("(p c) -> p c", c=PACK))
 
         def order_w2_words(g):
             cols = slice(g * KP, (g + 1) * KP)
-            nc.vector.tensor_copy(out=w2w[:].bitcast(U16)[:, cols].rearrange("p (t m) -> p m t", t=PACK),
-                                  in_=w2w_raw[:].bitcast(U16)[:, cols].rearrange("p (m t) -> p m t", t=PACK))
+            nc.vector.tensor_copy(out=w2w[:].bitcast(U16)[:, cols].rearrange("p (t m) -> p t m", t=PACK),
+                                  in_=w2w_raw[:].bitcast(U16)[:, cols].rearrange("p (m t) -> p t m", t=PACK))
 
         def order_w2_scales(g):
             cols = slice(g * KP, (g + 1) * KP)
-            nc.vector.tensor_copy(out=w2s[:, cols].rearrange("p (t m) -> p m t", t=PACK),
-                                  in_=w2s_raw[:].bitcast(U8)[:, cols].rearrange("p (m t) -> p m t", t=PACK))
+            nc.vector.tensor_copy(out=w2s[:, cols].rearrange("p (t m) -> p t m", t=PACK),
+                                  in_=w2s_raw[:].bitcast(U8)[:, cols].rearrange("p (m t) -> p t m", t=PACK))
 
         def gather(dst, window, offsets, j0, j1):
             nc.vector.tensor_copy(dst, window.indirect(offsets[:, j0 // 16:j1 // 16]))
@@ -133,11 +131,11 @@ def tile_list_inhibited_drug_response_kernel(tc, tab_words, tab_scales, tab2_wor
             v2w[j0] = held([P, j1 - j0], U32, f"v2w{j0}", place)
             gather(v2w[j0][:], t2w[:].bitcast(U32), list2, j0, j1)
 
-        def gather1s(t1s, h):
-            gather(v1s[h][:], t1s[:].bitcast(U8), list1, h * HALF, (h + 1) * HALF)
+        def gather1s(t1s):
+            gather(v1s[:], t1s[:].bitcast(U8), list1, 0, S)
 
-        def gather1w(a, h):
-            gather(v1w[a][h][:], t1w[a][:].bitcast(U32), list1, h * HALF, (h + 1) * HALF)
+        def gather1w(a):
+            gather(v1w[a][:], t1w[a][:].bitcast(U32), list1, 0, S)
 
         def round_copy(eng, dst, src):
             if eng == "v":
@@ -152,10 +150,10 @@ def tile_list_inhibited_drug_response_kernel(tc, tab_words, tab_scales, tab2_wor
 
         def cast(eng, raw):
             grouped = stage.tile([P, PACK * KP], BF16, name="grouped", bufs=4, align_bytes=64)
-            order = "p m j t" if eng == "v" else "p m t j"
+            order = "p m t j" if eng == "g" else "p m j t"
             dst = grouped[:].rearrange("p (t m j) -> " + order, t=PACK, j=PACK)
             src = raw[:].rearrange("p j (m t) -> " + order, t=PACK)
-            step = P if eng == "v" else P // 2
+            step = P // 2 if eng == "g" else P
             for m0 in range(0, P, step):
                 round_copy(eng, dst[:, m0:m0 + step], src[:, m0:m0 + step])
             return grouped
@@ -176,7 +174,7 @@ def tile_list_inhibited_drug_response_kernel(tc, tab_words, tab_scales, tab2_wor
                 bank = psum.tile([P, width], F32, name="by")
                 nc.tensor.matmul_mx(out=bank[:], lhsT=w2w[:, 2 * col:2 * (col + P)].bitcast(FP4X4),
                                     lhsT_scale=w2s[:, col:col + P], rhs=v2w[piece][:, cols].bitcast(FP8X4),
-                                    rhs_scale=v2s[piece][:, cols], start=True, stop=True)
+                                    rhs_scale=v2s[0][:, j0:j1], start=True, stop=True)
                 nc.scalar.activation(out=gate[g][h][:, t, c0:c0 + width], in_=bank[:], func=ACT.Abs,
                                      bias=bi_sb[:, g, t:t + 1])
 
@@ -191,20 +189,23 @@ def tile_list_inhibited_drug_response_kernel(tc, tab_words, tab_scales, tab2_wor
             part = gate_part(g, q)
             if SQ_ENG[4 * g + q] == "s":
                 nc.scalar.activation(out=part, in_=part, func=ACT.Square)
+            elif SQ_ENG[4 * g + q] == "g":
+                nc.gpsimd.tensor_tensor(out=part, in0=part, in1=part, op=ALU.mult)
             else:
                 nc.vector.tensor_tensor(out=part, in0=part, in1=part, op=ALU.mult)
 
-        def drive(g, q):
-            hb = stage.tile([P, YW * PACK], BF16, name="hb", bufs=3, align_bytes=64)
-            for u in range(YW // AW):
-                h, c0 = divmod(q * YW + u * AW, HALF)
+        def drive(g, j0, j1):
+            hb = stage.tile([P, (j1 - j0) * PACK], BF16, name="hb", bufs=3, align_bytes=64)
+            for u in range((j1 - j0) // AW):
+                j = j0 + u * AW
+                h, c0 = divmod(j, HALF)
                 bank = psum.tile([P, PACK, AW], F32, name="abank")
                 for t in range(PACK):
                     for a in range(2):
                         nc.tensor.matmul_mx(out=bank[:, t, :], lhsT=w1c[g][a][:, t * P:(t + 1) * P].bitcast(FP8X4),
                                             lhsT_scale=w1s[g][a][:, t * P:(t + 1) * P],
-                                            rhs=v1w[a][h][:, c0:c0 + AW].bitcast(FP8X4),
-                                            rhs_scale=v1s[h][TAB_ROW + 4 * a:, c0:c0 + AW],
+                                            rhs=v1w[a][:, j:j + AW].bitcast(FP8X4),
+                                            rhs_scale=v1s[TAB_ROW + 4 * a:, j:j + AW],
                                             start=(a == 0), stop=(a == 1))
                 nc.vector.tensor_tensor(
                     out=hb[:, u * AW * PACK:(u + 1) * AW * PACK].rearrange("p (c i t) -> p c t i", i=4, t=PACK),
@@ -213,103 +214,105 @@ def tile_list_inhibited_drug_response_kernel(tc, tab_words, tab_scales, tab2_wor
                     op=ALU.mult)
             return hb
 
-        def read_out(q):
-            res = stage.tile([P, N // P, YW], F32, name="res", bufs=3)
+        def quantize_h(g, j0, j1, hb):
+            nc.vector.quantize_mx(out=hc[g][:, j0:j1].bitcast(FP8X4), scales=hs[g][:, j0:j1], in_=hb[:])
+
+        def read_out(j0, j1, engines):
+            res = stage.tile([P, N // P, j1 - j0], F32, name="res", bufs=3)
             for pair in range(2):
-                bank = psum.tile([P, 2, YW], F32, name="by")
+                bank = psum.tile([P, 2, j1 - j0], F32, name="by")
                 for e in range(2):
                     c = 2 * pair + e
                     for g in range(2):
                         nc.tensor.matmul_mx(out=bank[:, e, :], lhsT=wrc[g][:, c * P:(c + 1) * P].bitcast(FP8X4),
                                             lhsT_scale=wrs[g][:, c * P:(c + 1) * P],
-                                            rhs=hc[g][q][:].bitcast(FP8X4), rhs_scale=hs[g][q][:],
+                                            rhs=hc[g][:, j0:j1].bitcast(FP8X4), rhs_scale=hs[g][:, j0:j1],
                                             start=(g == 0), stop=(g == 1))
                 for e in range(2):
                     c = 2 * pair + e
-                    if EVAC_ENG[2 * q + pair] == "s":
+                    if engines[pair] == "s":
                         nc.scalar.activation(out=res[:, c, :], in_=bank[:, e, :], func=ACT.Identity,
                                              bias=base_sb[:, c:c + 1])
                     else:
                         nc.vector.tensor_scalar(out=res[:, c, :], in0=bank[:, e, :], scalar1=base_sb[:, c:c + 1],
                                                 scalar2=None, op0=ALU.add)
                 nc.sync.dma_start(
-                    out=out[:, q * YW:(q + 1) * YW].rearrange("(p c) j -> p c j", c=PACK)[:, 2 * pair:2 * pair + 2, :],
+                    out=out[:, j0:j1].rearrange("(p c) j -> p c j", c=PACK)[:, 2 * pair:2 * pair + 2, :],
                     in_=res[:, 2 * pair:2 * pair + 2, :])
 
         load_t1w(0, 0)
-        order_w2_words(0)
-        order_w2_words(1)
         t1s = load_t1s(16384)
+        gather2s(0, 1024, None)
+        load_t1w(1, 28416)
+        order_w2_words(0)
         order_w2_scales(0)
-        gather2s(0, 256, None)
         gather2w(0, 256, None)
         load_gate(0, 0, 256)
+        order_w2_words(1)
         order_w2_scales(1)
-        load_t1w(1, 28416)
-        load_gate(1, 0, 256)
         root_gate(0, 0)
-        gather2s(256, 1024, 27648)
-        load_w1(0, 0, 45056)
-        gather2w(256, 1024, 24576)
-        load_w1(0, 1, 53248)
-        root_gate(1, 0)
+        load_w1(0, 0, 48128)
+        gather2w(256, 1024, 45056)
+        load_w1(0, 1, 56384)
+        load_gate(1, 0, 256)
         square_gate(0, 0)
-        square_gate(1, 0)
         load_gate(0, 256, 512)
-        load_gate(0, 512, 1024)
-        for h in range(2):
-            gather1w(0, h)
-        for h in range(2):
-            gather1s(t1s, h)
+        gather1w(0)
+        gather1s(t1s)
         load_w1(1, 0, 16384)
-        for h in range(2):
-            gather1w(1, h)
-        load_w1(1, 1, 28416)
+        gather1w(1)
+        root_gate(1, 0)
         root_gate(0, 1)
-        root_gate(0, 2)
+        square_gate(1, 0)
         square_gate(0, 1)
-        root_gate(0, 3)
         load_gate(1, 256, 512)
-        square_gate(0, 2)
-        square_gate(0, 3)
+        load_gate(0, 512, 1024)
         root_gate(1, 1)
-        load_gate(1, 512, 1024)
+        root_gate(0, 2)
         square_gate(1, 1)
+        square_gate(0, 2)
+        load_gate(1, 512, 1024)
+        root_gate(0, 3)
         root_gate(1, 2)
+        square_gate(0, 3)
         root_gate(1, 3)
         square_gate(1, 2)
         square_gate(1, 3)
         g00 = cast_w1(0, 0)
-        load_wr(0, 45056)
+        load_w1(1, 1, 48128)
         g01 = cast_w1(0, 1)
-        load_wr(1, 53248)
+        load_wr(0, 56320)
+        load_wr(1, 64512)
         quantize(w1c[0][0], w1s[0][0], g00)
         quantize(w1c[0][1], w1s[0][1], g01)
+        h0 = drive(0, 0, 256)
         g10 = cast_w1(1, 0)
-        g11 = cast_w1(1, 1)
-        h0 = drive(0, 0)
-        h1 = drive(0, 1)
-        quantize(hc[0][0], hs[0][0], h0)
-        h2 = drive(0, 2)
-        quantize(hc[0][1], hs[0][1], h1)
+        h1 = drive(0, 256, 512)
+        quantize_h(0, 0, 256, h0)
         quantize(w1c[1][0], w1s[1][0], g10)
-        h3 = drive(0, 3)
-        quantize(hc[0][2], hs[0][2], h2)
-        quantize(w1c[1][1], w1s[1][1], g11)
+        g11 = cast_w1(1, 1)
+        quantize_h(0, 256, 512, h1)
         r0 = cast_wr(0)
+        quantize(w1c[1][1], w1s[1][1], g11)
         r1 = cast_wr(1)
-        h0 = drive(1, 0)
-        quantize(hc[0][3], hs[0][3], h3)
         quantize(wrc[0], wrs[0], r0)
-        h1 = drive(1, 1)
-        quantize(hc[1][0], hs[1][0], h0)
+        h0 = drive(1, 0, 256)
         quantize(wrc[1], wrs[1], r1)
-        read_out(0)
-        h2 = drive(1, 2)
-        quantize(hc[1][1], hs[1][1], h1)
-        read_out(1)
-        h3 = drive(1, 3)
-        quantize(hc[1][2], hs[1][2], h2)
-        read_out(2)
-        quantize(hc[1][3], hs[1][3], h3)
-        read_out(3)
+        h1 = drive(1, 256, 512)
+        quantize_h(1, 0, 256, h0)
+        read_out(0, 256, "ss")
+        h2 = drive(0, 512, 768)
+        quantize_h(1, 256, 512, h1)
+        read_out(256, 512, "ss")
+        h3 = drive(1, 512, 768)
+        quantize_h(0, 512, 768, h2)
+        h4 = drive(0, 768, 1024)
+        quantize_h(1, 512, 768, h3)
+        read_out(512, 768, "ss")
+        h5 = drive(1, 768, 896)
+        quantize_h(0, 768, 1024, h4)
+        h6 = drive(1, 896, 1024)
+        quantize_h(1, 768, 896, h5)
+        read_out(768, 896, "ss")
+        quantize_h(1, 896, 1024, h6)
+        read_out(896, 1024, "sv")

@@ -23,7 +23,7 @@ HALF = 512
 AW = 128
 YW = 256
 TAB_ROW = 8
-CAST_ENG = "vvvvvv"
+CAST_ENG = ""
 SQ_ENG = "ssssssss"
 EVAC_ENG = ""
 
@@ -108,7 +108,8 @@ def tile_list_inhibited_drug_response_kernel(tc, tab_words, tab_scales, tab2_wor
         nc.sync.dma_start(out=w2w_raw[:], in_=w2_words[0].bitcast(I32))
         for q in range(4):
             load_scale_rows(nc.sync, w2s_raw, w2_scales[0], q)
-        nc.sync.dma_start(out=base_sb[:], in_=base.rearrange("(p c) -> p c", c=PACK))
+        with nc.allow_non_contiguous_dma(reason="one baseline value a partition"):
+            nc.sync.dma_start(out=base_sb[:], in_=base.rearrange("(c p) -> p c", p=P))
 
         def order_w2_words(g):
             cols = slice(g * KP, (g + 1) * KP)
@@ -148,21 +149,17 @@ def tile_list_inhibited_drug_response_kernel(tc, tab_words, tab_scales, tab2_wor
         def quantize(codes, scales, values):
             nc.vector.quantize_mx(out=codes[:].bitcast(FP8X4), scales=scales[:], in_=values[:])
 
-        def cast(eng, raw):
+        def cast_w1(g, a):
             grouped = stage.tile([P, PACK * KP], BF16, name="grouped", bufs=4, align_bytes=64)
-            order = "p m t j" if eng == "g" else "p m j t"
-            dst = grouped[:].rearrange("p (t m j) -> " + order, t=PACK, j=PACK)
-            src = raw[:].rearrange("p j (m t) -> " + order, t=PACK)
-            step = P // 2 if eng == "g" else P
-            for m0 in range(0, P, step):
-                round_copy(eng, dst[:, m0:m0 + step], src[:, m0:m0 + step])
+            nc.vector.tensor_copy(out=grouped[:].rearrange("p (u e m j) -> p u m j e", u=2, e=2, j=PACK),
+                                  in_=w1_raw[g, a][:].rearrange("p j (m u e) -> p u m j e", u=2, e=2))
             return grouped
 
-        def cast_w1(g, a):
-            return cast(CAST_ENG[2 * g + a], w1_raw[g, a])
-
         def cast_wr(g):
-            return cast(CAST_ENG[4 + g], wr_raw[g])
+            grouped = stage.tile([P, PACK * N], BF16, name="grouped", bufs=4, align_bytes=64)
+            nc.vector.tensor_copy(out=grouped[:].rearrange("p (c i j) -> p c j i", i=2, j=PACK),
+                                  in_=wr_raw[g][:].rearrange("p j (c i) -> p c j i", i=2))
+            return grouped
 
         def load_gate(g, j0, j1):
             h, c0 = divmod(j0, HALF)
@@ -208,9 +205,9 @@ def tile_list_inhibited_drug_response_kernel(tc, tab_words, tab_scales, tab2_wor
                                             rhs_scale=v1s[TAB_ROW + 4 * a:, j:j + AW],
                                             start=(a == 0), stop=(a == 1))
                 nc.vector.tensor_tensor(
-                    out=hb[:, u * AW * PACK:(u + 1) * AW * PACK].rearrange("p (c i t) -> p c t i", i=4, t=PACK),
-                    in0=bank[:].rearrange("p t (c i) -> p c t i", i=4),
-                    in1=gate[g][h][:, :, c0:c0 + AW].rearrange("p t (c i) -> p c t i", i=4),
+                    out=hb[:, u * AW * PACK:(u + 1) * AW * PACK].rearrange("p (c i t) -> p c t i", i=2, t=PACK),
+                    in0=bank[:].rearrange("p t (c i) -> p c t i", i=2),
+                    in1=gate[g][h][:, :, c0:c0 + AW].rearrange("p t (c i) -> p c t i", i=2),
                     op=ALU.mult)
             return hb
 
@@ -237,7 +234,7 @@ def tile_list_inhibited_drug_response_kernel(tc, tab_words, tab_scales, tab2_wor
                         nc.vector.tensor_scalar(out=res[:, c, :], in0=bank[:, e, :], scalar1=base_sb[:, c:c + 1],
                                                 scalar2=None, op0=ALU.add)
                 nc.sync.dma_start(
-                    out=out[:, j0:j1].rearrange("(p c) j -> p c j", c=PACK)[:, 2 * pair:2 * pair + 2, :],
+                    out=out[2 * pair * P:(2 * pair + 2) * P, j0:j1].rearrange("(e p) j -> p e j", p=P),
                     in_=res[:, 2 * pair:2 * pair + 2, :])
 
         load_t1w(0, 0)

@@ -156,9 +156,13 @@ def tile_list_inhibited_drug_response_kernel(tc, tab_words, tab_scales, tab2_wor
             return grouped
 
         def cast_wr(g):
-            grouped = stage.tile([P, PACK * N], BF16, name="grouped", bufs=4, align_bytes=64)
-            nc.vector.tensor_copy(out=grouped[:].rearrange("p (c i j) -> p c j i", i=2, j=PACK),
-                                  in_=wr_raw[g][:].rearrange("p j (c i) -> p c j i", i=2))
+            if g == 0:
+                grouped = stage.tile([P, PACK * N], BF16, name="grouped", bufs=4, align_bytes=64)
+            else:
+                grouped = held([P, PACK * N], BF16, "wr1_grouped", 0)
+            copy = nc.vector.tensor_copy if g == 0 else nc.scalar.copy
+            copy(out=grouped[:].rearrange("p (c i j) -> p c j i", i=2, j=PACK),
+                 in_=wr_raw[g][:].rearrange("p j (c i) -> p c j i", i=2))
             return grouped
 
         def load_gate(g, j0, j1):
@@ -191,8 +195,11 @@ def tile_list_inhibited_drug_response_kernel(tc, tab_words, tab_scales, tab2_wor
             else:
                 nc.vector.tensor_tensor(out=part, in0=part, in1=part, op=ALU.mult)
 
-        def drive(g, j0, j1):
-            hb = stage.tile([P, (j1 - j0) * PACK], BF16, name="hb", bufs=3, align_bytes=64)
+        def drive(g, j0, j1, place=None):
+            if place is None:
+                hb = stage.tile([P, (j1 - j0) * PACK], BF16, name="hb", bufs=3, align_bytes=64)
+            else:
+                hb = held([P, (j1 - j0) * PACK], BF16, f"hb{g}_{j0}", place)
             for u in range((j1 - j0) // AW):
                 j = j0 + u * AW
                 h, c0 = divmod(j, HALF)
@@ -252,18 +259,18 @@ def tile_list_inhibited_drug_response_kernel(tc, tab_words, tab_scales, tab2_wor
         gather2w(256, 1024, 45056)
         load_w1(0, 1, 56384)
         load_gate(1, 0, 256)
-        square_gate(0, 0)
+        root_gate(1, 0)
         load_gate(0, 256, 512)
         gather1w(0)
         gather1s(t1s)
         load_w1(1, 0, 16384)
+        square_gate(0, 0)
         gather1w(1)
-        root_gate(1, 0)
-        root_gate(0, 1)
         square_gate(1, 0)
-        square_gate(0, 1)
         load_gate(1, 256, 512)
+        root_gate(0, 1)
         load_gate(0, 512, 1024)
+        square_gate(0, 1)
         root_gate(1, 1)
         root_gate(0, 2)
         square_gate(1, 1)
@@ -272,14 +279,15 @@ def tile_list_inhibited_drug_response_kernel(tc, tab_words, tab_scales, tab2_wor
         root_gate(0, 3)
         root_gate(1, 2)
         square_gate(0, 3)
-        root_gate(1, 3)
         square_gate(1, 2)
-        square_gate(1, 3)
         g00 = cast_w1(0, 0)
         load_w1(1, 1, 48128)
         g01 = cast_w1(0, 1)
         load_wr(0, 56320)
         load_wr(1, 64512)
+        r1 = cast_wr(1)
+        root_gate(1, 3)
+        square_gate(1, 3)
         quantize(w1c[0][0], w1s[0][0], g00)
         quantize(w1c[0][1], w1s[0][1], g01)
         h0 = drive(0, 0, 256)
@@ -291,25 +299,24 @@ def tile_list_inhibited_drug_response_kernel(tc, tab_words, tab_scales, tab2_wor
         quantize_h(0, 256, 512, h1)
         r0 = cast_wr(0)
         quantize(w1c[1][1], w1s[1][1], g11)
-        r1 = cast_wr(1)
+        h2 = drive(0, 512, 768)
         quantize(wrc[0], wrs[0], r0)
         h0 = drive(1, 0, 256)
-        quantize(wrc[1], wrs[1], r1)
+        quantize_h(0, 512, 768, h2)
         h1 = drive(1, 256, 512)
         quantize_h(1, 0, 256, h0)
+        quantize(wrc[1], wrs[1], r1)
         read_out(0, 256, "ss")
-        h2 = drive(0, 512, 768)
         quantize_h(1, 256, 512, h1)
         read_out(256, 512, "ss")
-        h3 = drive(1, 512, 768)
-        quantize_h(0, 512, 768, h2)
-        h4 = drive(0, 768, 1024)
+        h3 = drive(1, 512, 768, 0)
+        h4 = drive(0, 768, 1024, 2048)
         quantize_h(1, 512, 768, h3)
         read_out(512, 768, "ss")
         h5 = drive(1, 768, 896)
         quantize_h(0, 768, 1024, h4)
         h6 = drive(1, 896, 1024)
         quantize_h(1, 768, 896, h5)
-        read_out(768, 896, "ss")
+        read_out(768, 896, "sv")
         quantize_h(1, 896, 1024, h6)
         read_out(896, 1024, "sv")

from contextlib import ExitStack

import concourse.mybir as mybir

K, K2, H, N, T, T2, S = 1024, 512, 1024, 512, 4096, 2048, 1024
FLOPS = 2 * (K * H * S + K2 * H * S + H * N * S)

F32 = mybir.dt.float32
BF16 = mybir.dt.bfloat16
I32 = mybir.dt.int32
U32 = mybir.dt.uint32
U16 = mybir.dt.uint16
U8 = mybir.dt.uint8
FP8X4 = mybir.dt.float8_e4m3fn_x4
FP4X4 = mybir.dt.float4_e2m1fn_x4
ACT = mybir.ActivationFunctionType
ALU = mybir.AluOpType

P = 128
PACK = 4
KP = P * PACK
HALF = 512
AW = 128
YW = 256
TAB_ROW = 8
CAST_ENG = ""
SQ_ENG = "ssssssss"
EVAC_ENG = ""


def tile_list_inhibited_drug_response_kernel(tc, tab_words, tab_scales, tab2_words, tab2_scales, offs, offs2,
                                                      w1, w2_words, w2_scales, bi, wr, base, out):
    nc = tc.nc
    with ExitStack() as ctx:
        keep = ctx.enter_context(tc.tile_pool(name="keep", bufs=1))
        ring = ctx.enter_context(tc.tile_pool(name="ring", bufs=1))
        stage = ctx.enter_context(tc.tile_pool(name="stage", bufs=2))
        psum = ctx.enter_context(tc.psum_pool(name="psum", bufs=4))

        def held(shape, dtype, name, place=None):
            if place is None:
                return keep.tile(shape, dtype, name=name, align_bytes=64)
            return ring.tile(shape, dtype, name=name, align_bytes=64, offset=place)

        list1 = held([P, S // 16], U16, "list1")
        list2 = held([P, S // 16], U16, "list2")
        w2w_raw = held([P, H // 2], I32, "w2w_raw")
        w2s_raw = held([P, H // 4], I32, "w2s_raw", 48064)
        t2s = held([P, T2 // 4], I32, "t2s", 28416)
        t2w = held([P, T2], I32, "t2w", 56384)
        w2w = held([P, 2 * H], U8, "w2w")
        w2s = held([P, H], U8, "w2s")
        bi_sb = held([P, 2, PACK], F32, "bi_sb")
        base_sb = held([P, N // P], F32, "base_sb")
        warm = held([P, 32], F32, "warm", 16320)
        t1w, w1_raw, wr_raw = {}, {}, {}
        w1c = [[held([P, KP], U32, f"w1c{g}{a}") for a in range(2)] for g in range(2)]
        w1s = [[held([P, KP], U8, f"w1s{g}{a}") for a in range(2)] for g in range(2)]
        wrc = [held([P, N], U32, f"wrc{g}") for g in range(2)]
        wrs = [held([P, N], U8, f"wrs{g}") for g in range(2)]
        v2w, v2s = {}, {}
        v1w = [held([P, S], U32, f"v1w{a}") for a in range(2)]
        v1s = held([P, S], U8, "v1s")
        gate = [[held([P, PACK, HALF], F32, f"gate{g}{h}") for h in range(2)] for g in range(2)]
        hc = [held([P, S], U32, f"hc{g}") for g in range(2)]
        hs = [held([P, S], U8, f"hs{g}") for g in range(2)]

        nc.vector.memset(t2s[:], 0)
        nc.vector.memset(warm[:], 1.0)
        nc.vector.memset(w2s_raw[:], 0)
        nc.scalar.activation(out=warm[:], in_=warm[:], func=ACT.Abs_reciprocal_sqrt)

        def load_scale_rows(queue, tile, rows, q):
            queue.dma_start(out=tile[32 * q:32 * q + 4, :], in_=rows[4 * q:4 * q + 4, :].bitcast(I32))

        def load_words(tile, words):
            nc.sync.dma_start(out=tile[:], in_=words.rearrange("p t i -> p (t i)").bitcast(I32))

        def load_rows(tile, rows):
            nc.sync.dma_start(out=tile[:], in_=rows.rearrange("(p j) c -> p j c", j=PACK))

        def load_t1w(a, slot):
            t1w[a] = held([P, T], I32, f"t1w{a}", slot)
            load_words(t1w[a], tab_words[a])

        def load_t1s(slot):
            tile = held([P, T // 4], I32, "t1s", slot)
            nc.vector.memset(tile[:], 0)
            for q in range(4):
                p0 = 32 * q + TAB_ROW
                nc.sync.dma_start(out=tile[p0:p0 + 8, :], in_=tab_scales[:, 4 * q:4 * q + 4, :].bitcast(I32))
            return tile

        def load_w1(g, a, slot):
            w1_raw[g, a] = held([P, PACK, KP], F32, f"w1raw{g}{a}", slot)
            load_rows(w1_raw[g, a], w1[a * KP:(a + 1) * KP, g * KP:(g + 1) * KP])

        def load_wr(g, slot):
            wr_raw[g] = held([P, PACK, N], F32, f"wrraw{g}", slot)
            load_rows(wr_raw[g], wr[g * KP:(g + 1) * KP, :])

        nc.sync.dma_start(list2[:], offs2)
        nc.sync.dma_start(list1[:], offs)
        nc.sync.dma_start(out=bi_sb[:], in_=bi.rearrange("(g p t) -> p g t", g=2, t=PACK))
        for q in range(4):
            load_scale_rows(nc.sync, t2s, tab2_scales[0], q)
        load_words(t2w, tab2_words[0])
        nc.sync.dma_start(out=w2w_raw[:], in_=w2_words[0].bitcast(I32))
        for q in range(4):
            load_scale_rows(nc.sync, w2s_raw, w2_scales[0], q)
        with nc.allow_non_contiguous_dma(reason="one baseline value a partition"):
            nc.sync.dma_start(out=base_sb[:], in_=base.rearrange("(c p) -> p c", p=P))

        def order_w2_words(g):
            cols = slice(g * KP, (g + 1) * KP)
            nc.vector.tensor_copy(out=w2w[:].bitcast(U16)[:, cols].rearrange("p (t m) -> p t m", t=PACK),
                                  in_=w2w_raw[:].bitcast(U16)[:, cols].rearrange("p (m t) -> p t m", t=PACK))

        def order_w2_scales(g):
            cols = slice(g * KP, (g + 1) * KP)
            nc.vector.tensor_copy(out=w2s[:, cols].rearrange("p (t m) -> p t m", t=PACK),
                                  in_=w2s_raw[:].bitcast(U8)[:, cols].rearrange("p (m t) -> p t m", t=PACK))

        def gather(dst, window, offsets, j0, j1):
            nc.vector.tensor_copy(dst, window.indirect(offsets[:, j0 // 16:j1 // 16]))

        def gather2s(j0, j1, place):
            v2s[j0] = held([P, j1 - j0], U8, f"v2s{j0}", place)
            gather(v2s[j0][:], t2s[:].bitcast(U8), list2, j0, j1)

        def gather2w(j0, j1, place):
            v2w[j0] = held([P, j1 - j0], U32, f"v2w{j0}", place)
            gather(v2w[j0][:], t2w[:].bitcast(U32), list2, j0, j1)

        def gather1s(t1s):
            gather(v1s[:], t1s[:].bitcast(U8), list1, 0, S)

        def gather1w(a):
            gather(v1w[a][:], t1w[a][:].bitcast(U32), list1, 0, S)

        def round_copy(eng, dst, src):
            if eng == "v":
                nc.vector.tensor_copy(out=dst, in_=src)
            elif eng == "s":
                nc.scalar.copy(out=dst, in_=src)
            else:
                nc.gpsimd.tensor_scalar(out=dst, in0=src, scalar1=1.0, scalar2=0.0, op0=ALU.mult, op1=ALU.add)

        def quantize(codes, scales, values):
            nc.vector.quantize_mx(out=codes[:].bitcast(FP8X4), scales=scales[:], in_=values[:])

        def cast_w1(g, a):
            grouped = stage.tile([P, PACK * KP], BF16, name="grouped", bufs=4, align_bytes=64)
            nc.vector.tensor_copy(out=grouped[:].rearrange("p (u e m j) -> p u m j e", u=2, e=2, j=PACK),
                                  in_=w1_raw[g, a][:].rearrange("p j (m u e) -> p u m j e", u=2, e=2))
            return grouped

        def cast_wr(g):
            if g == 0:
                grouped = stage.tile([P, PACK * N], BF16, name="grouped", bufs=4, align_bytes=64)
            else:
                grouped = held([P, PACK * N], BF16, "wr1_grouped", 0)
            copy = nc.vector.tensor_copy if g == 0 else nc.scalar.copy
            copy(out=grouped[:].rearrange("p (c i j) -> p c j i", i=2, j=PACK),
                 in_=wr_raw[g][:].rearrange("p j (c i) -> p c j i", i=2))
            return grouped

        def load_gate(g, j0, j1):
            h, c0 = divmod(j0, HALF)
            width = j1 - j0
            piece = 0 if j0 < YW else YW
            cols = slice(j0 - piece, j1 - piece)
            for t in range(PACK):
                col = g * KP + t * P
                bank = psum.tile([P, width], F32, name="by")
                nc.tensor.matmul_mx(out=bank[:], lhsT=w2w[:, 2 * col:2 * (col + P)].bitcast(FP4X4),
                                    lhsT_scale=w2s[:, col:col + P], rhs=v2w[piece][:, cols].bitcast(FP8X4),
                                    rhs_scale=v2s[0][:, j0:j1], start=True, stop=True)
                nc.scalar.activation(out=gate[g][h][:, t, c0:c0 + width], in_=bank[:], func=ACT.Abs,
                                     bias=bi_sb[:, g, t:t + 1])

        def gate_part(g, q):
            h, c0 = divmod(q * YW, HALF)
            return gate[g][h][:, :, c0:c0 + YW]

        def root_gate(g, q):
            nc.scalar.activation(out=gate_part(g, q), in_=gate_part(g, q), func=ACT.Abs_reciprocal_sqrt, bias=1.0)

        def square_gate(g, q):
            part = gate_part(g, q)
            if SQ_ENG[4 * g + q] == "s":
                nc.scalar.activation(out=part, in_=part, func=ACT.Square)
            elif SQ_ENG[4 * g + q] == "g":
                nc.gpsimd.tensor_tensor(out=part, in0=part, in1=part, op=ALU.mult)
            else:
                nc.vector.tensor_tensor(out=part, in0=part, in1=part, op=ALU.mult)

        def drive(g, j0, j1, place=None):
            if place is None:
                hb = stage.tile([P, (j1 - j0) * PACK], BF16, name="hb", bufs=3, align_bytes=64)
            else:
                hb = held([P, (j1 - j0) * PACK], BF16, f"hb{g}_{j0}", place)
            for u in range((j1 - j0) // AW):
                j = j0 + u * AW
                h, c0 = divmod(j, HALF)
                bank = psum.tile([P, PACK, AW], F32, name="abank")
                for t in range(PACK):
                    for a in range(2):
                        nc.tensor.matmul_mx(out=bank[:, t, :], lhsT=w1c[g][a][:, t * P:(t + 1) * P].bitcast(FP8X4),
                                            lhsT_scale=w1s[g][a][:, t * P:(t + 1) * P],
                                            rhs=v1w[a][:, j:j + AW].bitcast(FP8X4),
                                            rhs_scale=v1s[TAB_ROW + 4 * a:, j:j + AW],
                                            start=(a == 0), stop=(a == 1))
                nc.vector.tensor_tensor(
                    out=hb[:, u * AW * PACK:(u + 1) * AW * PACK].rearrange("p (c i t) -> p c t i", i=2, t=PACK),
                    in0=bank[:].rearrange("p t (c i) -> p c t i", i=2),
                    in1=gate[g][h][:, :, c0:c0 + AW].rearrange("p t (c i) -> p c t i", i=2),
                    op=ALU.mult)
            return hb

        def quantize_h(g, j0, j1, hb):
            nc.vector.quantize_mx(out=hc[g][:, j0:j1].bitcast(FP8X4), scales=hs[g][:, j0:j1], in_=hb[:])

        def read_out(j0, j1, engines):
            res = stage.tile([P, N // P, j1 - j0], F32, name="res", bufs=3)
            for pair in range(2):
                bank = psum.tile([P, 2, j1 - j0], F32, name="by")
                for e in range(2):
                    c = 2 * pair + e
                    for g in range(2):
                        nc.tensor.matmul_mx(out=bank[:, e, :], lhsT=wrc[g][:, c * P:(c + 1) * P].bitcast(FP8X4),
                                            lhsT_scale=wrs[g][:, c * P:(c + 1) * P],
                                            rhs=hc[g][:, j0:j1].bitcast(FP8X4), rhs_scale=hs[g][:, j0:j1],
                                            start=(g == 0), stop=(g == 1))
                for e in range(2):
                    c = 2 * pair + e
                    if engines[pair] == "s":
                        nc.scalar.activation(out=res[:, c, :], in_=bank[:, e, :], func=ACT.Identity,
                                             bias=base_sb[:, c:c + 1])
                    else:
                        nc.vector.tensor_scalar(out=res[:, c, :], in0=bank[:, e, :], scalar1=base_sb[:, c:c + 1],
                                                scalar2=None, op0=ALU.add)
                nc.sync.dma_start(
                    out=out[2 * pair * P:(2 * pair + 2) * P, j0:j1].rearrange("(e p) j -> p e j", p=P),
                    in_=res[:, 2 * pair:2 * pair + 2, :])

        load_t1w(0, 0)
        t1s = load_t1s(16384)
        gather2s(0, 1024, None)
        load_t1w(1, 28416)
        order_w2_words(0)
        order_w2_scales(0)
        gather2w(0, 256, None)
        load_gate(0, 0, 256)
        order_w2_words(1)
        order_w2_scales(1)
        root_gate(0, 0)
        load_w1(0, 0, 48128)
        gather2w(256, 1024, 45056)
        load_w1(0, 1, 56384)
        load_gate(1, 0, 256)
        root_gate(1, 0)
        load_gate(0, 256, 512)
        gather1w(0)
        gather1s(t1s)
        load_w1(1, 0, 16384)
        square_gate(0, 0)
        gather1w(1)
        square_gate(1, 0)
        load_gate(1, 256, 512)
        root_gate(0, 1)
        load_gate(0, 512, 1024)
        square_gate(0, 1)
        root_gate(1, 1)
        root_gate(0, 2)
        square_gate(1, 1)
        square_gate(0, 2)
        load_gate(1, 512, 1024)
        root_gate(0, 3)
        root_gate(1, 2)
        square_gate(0, 3)
        square_gate(1, 2)
        g00 = cast_w1(0, 0)
        load_w1(1, 1, 48128)
        g01 = cast_w1(0, 1)
        load_wr(0, 56320)
        load_wr(1, 64512)
        r1 = cast_wr(1)
        root_gate(1, 3)
        square_gate(1, 3)
        quantize(w1c[0][0], w1s[0][0], g00)
        quantize(w1c[0][1], w1s[0][1], g01)
        h0 = drive(0, 0, 256)
        g10 = cast_w1(1, 0)
        h1 = drive(0, 256, 512)
        quantize_h(0, 0, 256, h0)
        quantize(w1c[1][0], w1s[1][0], g10)
        g11 = cast_w1(1, 1)
        quantize_h(0, 256, 512, h1)
        r0 = cast_wr(0)
        quantize(w1c[1][1], w1s[1][1], g11)
        h2 = drive(0, 512, 768)
        quantize(wrc[0], wrs[0], r0)
        h0 = drive(1, 0, 256)
        quantize_h(0, 512, 768, h2)
        h1 = drive(1, 256, 512)
        quantize_h(1, 0, 256, h0)
        quantize(wrc[1], wrs[1], r1)
        read_out(0, 256, "ss")
        quantize_h(1, 256, 512, h1)
        read_out(256, 512, "ss")
        h3 = drive(1, 512, 768, 0)
        h4 = drive(0, 768, 1024, 2048)
        quantize_h(1, 512, 768, h3)
        read_out(512, 768, "ss")
        h5 = drive(1, 768, 896)
        quantize_h(0, 768, 1024, h4)
        h6 = drive(1, 896, 1024)
        quantize_h(1, 768, 896, h5)
        read_out(768, 896, "sv")
        quantize_h(1, 896, 1024, h6)
        read_out(896, 1024, "sv")
